import numpy as np, ml_dtypes
CORES = [23,119,17,113]
N = 4
GR, GC = 2, 2
L, KA, KB, F = 4, 2, 2, 64
def setup_inputs(rng):
    return {"a": rng.standard_normal((N, 128, KA * 128), dtype=np.float32).astype(ml_dtypes.bfloat16), "b": rng.standard_normal((N, 128, KB * F), dtype=np.float32).astype(ml_dtypes.bfloat16)}
def setup_inputs_big(rng):
    d = setup_inputs(rng)
    for k in ("a", "b"): d[k] = (d[k].astype(np.float32) * 1024.0).astype(d[k].dtype)
    return d
def setup_inputs_small(rng):
    d = setup_inputs(rng)
    for k in ("a", "b"): d[k] = (d[k].astype(np.float32) * (1 / 1024.0)).astype(d[k].dtype)
    return d
def setup_inputs_apart(rng):
    d = setup_inputs(rng)
    f = (10.0 ** rng.permutation(np.linspace(-1.5, 1.5, N))).astype(np.float32).reshape(N, 1, 1)
    for k in ("a", "b"): d[k] = (d[k].astype(np.float32) * f).astype(d[k].dtype)
    return d
def reference(a, b):
    A, B = a.astype(np.float64), b.astype(np.float64)
    y = np.zeros((N, 128, F))
    for i in range(GR):
        for j in range(GC):
            for k in range(L):
                At = A[i * GC + k // KA][:, 128 * (k % KA):128 * (k % KA) + 128]
                Bt = B[(k // KB) * GC + j][:, F * (k % KB):F * (k % KB) + F]
                y[i * GC + j] += At.T @ Bt
    return {"y": y.astype(ml_dtypes.bfloat16 if a.dtype != np.float64 else np.float64)}

GR, GC = 2, 2
L, KA, KB, F = 4, 2, 2, 64
P = 128

SCRATCH = {
    "a_own": ("sbuf", [P, KA * P], "bfloat16"),
    "b_own": ("sbuf", [P, KB * F], "bfloat16"),
    "a_in": ("sbuf", [P, KA * P], "bfloat16"),
    "b_in": ("sbuf", [P, KB * F], "bfloat16"),
    "acc": ("psum", [P, F], "float32"),
    "y_sb": ("sbuf", [P, F], "bfloat16"),
}
SEMAPHORES = ["a_ld", "b_ld", "a_arr", "b_arr", "sent", "mm", "cp", "st"]


def _count(mask):
    return bin(mask).count("1")


def rank_program(g, core, T, topo):
    rank = T.rank_of(core)
    if rank is None:
        return
    i, j = divmod(rank, GC)
    row_mate = T.cores[i * GC + (1 - j)]
    col_mate = T.cores[(1 - i) * GC + j]
    for dst in (row_mate, col_mate):
        if not topo.may_write(core, dst):
            raise ValueError("core %d may not write to core %d" % (core, dst))
    s = T.sem

    g.sync.dma_start(T.a_own[:], T.a[:, :]).then_inc(s.a_ld, 16)
    g.scalar.dma_start(T.b_own[:], T.b[:, :]).then_inc(s.b_ld, 16)

    a_mask = topo.mask(core, row_mate)
    b_mask = topo.mask(core, col_mate) & a_mask
    rid, pid, _ = topo.addr(row_mate)
    g.wait_ge(s.a_ld, 16)
    g.remote_dma(T.a_in[:], T.a_own[:], s.a_arr, s.sent, pid, rid, a_mask)
    rid, pid, _ = topo.addr(col_mate)
    g.wait_ge(s.b_ld, 16)
    g.remote_dma(T.b_in[:], T.b_own[:], s.b_arr, s.sent, pid, rid, b_mask)

    terms = []
    for k in range(L):
        a_far = (k // KA) != j
        b_far = (k // KB) != i
        terms.append((2 * a_far + b_far, k, a_far, b_far))
    terms.sort()
    te = g.tensor
    te.wait_ge(s.a_ld, 16)
    te.wait_ge(s.b_ld, 16)
    waited = {"a": False, "b": False}
    for n, (_, k, a_far, b_far) in enumerate(terms):
        if b_far and not waited["b"]:
            te.wait_ge(s.b_arr, _count(b_mask))
            waited["b"] = True
        if a_far and not waited["a"]:
            te.wait_ge(s.a_arr, _count(a_mask))
            waited["a"] = True
        ta, tb = k % KA, k % KB
        lhsT = (T.a_in if a_far else T.a_own)[:, P * ta:P * ta + P]
        rhs = (T.b_in if b_far else T.b_own)[:, F * tb:F * tb + F]
        mm = te.matmul(T.acc[:], lhsT, rhs, start=(n == 0), stop=(n == L - 1))
        if n == L - 1:
            mm.then_inc(s.mm, 1)

    g.vector.wait_ge(s.mm, 1)
    g.vector.tensor_copy(T.y_sb[:], T.acc[:]).then_inc(s.cp, 1)
    g.sync.wait_ge(s.cp, 1)
    g.sync.dma_start(T.y[:, :], T.y_sb[:]).then_inc(s.st, 16)
    g.sync.wait_ge(s.st, 16)

    g.wait_ge(s.sent, _count(a_mask) + _count(b_mask))
